import numpy as np
import ml_dtypes


def mxq(x, axis, fmt="e4m3"):
    dtype, down = {"e4m3": (ml_dtypes.float8_e4m3fn, 7), "e5m2": (ml_dtypes.float8_e5m2, 14)}[fmt]
    v = np.moveaxis(np.asarray(x, np.float32).astype(ml_dtypes.bfloat16).astype(np.float64), axis, -1)
    blocks = v.reshape(v.shape[:-1] + (-1, 32))
    amax = np.abs(blocks).max(-1, keepdims=True)
    byte = np.maximum(np.where(amax > 0, np.frexp(amax)[1] - 1 + 127, 0) - down, 1)
    scale = np.exp2(byte - 127.0)
    codes = (blocks / scale).astype(np.float32).astype(dtype).astype(np.float64)
    return np.moveaxis((codes * scale).reshape(v.shape), -1, axis)


WIDE = False


def mx_kscale(k):
    if not WIDE:
        return np.ones(k)
    levels = np.array([10, -10, 5, -5, 0])
    if k % 512:
        return np.exp2(np.random.permutation(np.resize(levels, k // 32))).repeat(32)
    a = np.empty((k // 512, 16))
    for p in range(k // 512):
        a[p, :8] = np.random.permutation(np.resize(levels, 8))
        for g in range(8):
            far = levels[np.abs(levels - a[p, g]) >= 10]
            a[p, g + 8] = far[np.random.randint(len(far))]
    return np.exp2(a.ravel()).repeat(32)


def f64(x):
    return np.asarray(x).astype(np.float64)


def striped(idx):
    return np.tile(idx.reshape(-1, 16).T, (8, 1)).astype(np.uint16)


def unstriped(offs):
    return offs[:16].T.reshape(-1).astype(np.int64)


E2M1 = np.array([0.0, 0.5, 1.0, 1.5, 2.0, 3.0, 4.0, 6.0, -0.0, -0.5, -1.0, -1.5, -2.0, -3.0, -4.0, -6.0])


def pack_weight(w, fmt):
    k, n = w.shape
    w = f64(np.asarray(w, np.float32).astype(ml_dtypes.bfloat16)).reshape(k // 32, 32, n)
    amax = np.abs(w).max(1)
    if fmt == "e4m3":
        byte = np.frexp(amax)[1] - 1 + 127 - 7
    else:
        mant, ex = np.frexp(amax / 6.0)
        byte = np.where(mant > 0.5, ex, ex - 1) + 127
    byte = np.clip(np.where(amax > 0, byte, 1), 1, 254)
    scaled = (w * np.exp2(127.0 - byte)[:, None, :]).reshape(k, n).astype(np.float32)
    by_word = np.ascontiguousarray(scaled.reshape(k // 512, 128, 4, n).transpose(0, 1, 3, 2))
    if fmt == "e4m3":
        words = by_word.astype(ml_dtypes.float8_e4m3fn).view(np.uint8)
    else:
        c = by_word.astype(ml_dtypes.float4_e2m1fn).view(np.uint8) & 0xF
        words = (c[..., 0::2] | (c[..., 1::2] << 4)).reshape(k // 512, 128, 2 * n)
    return np.ascontiguousarray(words), np.ascontiguousarray(byte.astype(np.uint8).reshape(k // 512, 16, n))


def unpack_weight(words, scales, fmt):
    g, _, n = scales.shape
    words = np.ascontiguousarray(words).reshape(g, 128, n, -1)
    if fmt == "e4m3":
        vals = words.view(ml_dtypes.float8_e4m3fn).astype(np.float64)
    else:
        nib = np.empty((g, 128, n, 4), np.uint8)
        nib[..., 0::2] = words & 0xF
        nib[..., 1::2] = words >> 4
        vals = E2M1[nib]
    vals = vals * np.repeat(np.exp2(scales.astype(np.float64) - 127.0), 8, axis=1)[..., None]
    return vals.transpose(0, 1, 3, 2).reshape(g * 512, n)


def gelu(v):
    return 0.5 * v * (1.0 + np.tanh(np.sqrt(2.0 / np.pi) * (v + 0.044715 * v**3)))


K, T, S, H, T3, S2, P = 512, 4096, 1024, 1024, 2048, 1024, 512

def setup_inputs():
    n = np.random.standard_normal
    s = mx_kscale(K)[:, None]
    u = mx_kscale(H)[:, None]
    tab_words, tab_scales = pack_weight(n((K, T)) * s, "e4m3")
    tab2_words, tab2_scales = pack_weight(n((H, T3)) / u / np.sqrt(H), "e4m3")
    w4_words, w4_scales = pack_weight(n((K, H)) / s / np.sqrt(K), "e2m1")
    return {
        "tab_words": tab_words, "tab_scales": tab_scales,
        "offs": striped(np.random.permutation(T)[:S]),
        "tab2_words": tab2_words, "tab2_scales": tab2_scales,
        "offs2": striped(np.random.permutation(T3)[:S2]),
        "pos1": striped(np.random.permutation(S)[:P]),
        "pos2": striped(np.random.permutation(S)[:P]),
        "w1": (n((K, H)) / s / np.sqrt(K)).astype(np.float32),
        "w4_words": w4_words, "w4_scales": w4_scales,
        "gain": (np.exp(0.3 * n(H)) * u[:, 0]).astype(np.float32),
        "lunch": (0.7 * n(H) * u[:, 0]).astype(np.float32),
        "base": (0.6 * n(S2)).astype(np.float32),
    }

def reference(tab_words, tab_scales, offs, tab2_words, tab2_scales, offs2, pos1, pos2,
              w1, w4_words, w4_scales, gain, lunch, base):
    v = unpack_weight(tab_words, tab_scales, "e4m3")[:, unstriped(offs)]
    v2 = unpack_weight(tab2_words, tab2_scales, "e4m3")[:, unstriped(offs2)]
    w4 = unpack_weight(w4_words, w4_scales, "e2m1")
    d1 = mxq(f64(w1), 0, "e4m3").T @ v
    d2 = w4.T @ v
    h = f64(gain)[:, None] * np.maximum(d1, d2)
    x1 = mxq(h[:, unstriped(pos1)] + f64(lunch)[:, None], 0, "e4m3")
    x2 = mxq(np.abs(h[:, unstriped(pos2)]), 0, "e4m3")
    e1 = v2.T @ x1
    e2 = v2.T @ x2
    return np.maximum(e1, e2) + f64(base)[:, None]

@@ -1,0 +1,301 @@
+from contextlib import ExitStack
+
+import concourse.mybir as mybir
+
+K, T, S, H, T2, S2, N = 512, 4096, 1024, 1024, 2048, 1024, 512
+FLOPS = 2 * (2 * K * H * S) + 2 * (2 * H * S2 * N)
+
+F32 = mybir.dt.float32
+BF16 = mybir.dt.bfloat16
+I32 = mybir.dt.int32
+U32 = mybir.dt.uint32
+U16 = mybir.dt.uint16
+U8 = mybir.dt.uint8
+FP8X4 = mybir.dt.float8_e4m3fn_x4
+FP4X4 = mybir.dt.float4_e2m1fn_x4
+ACT = mybir.ActivationFunctionType
+ALU = mybir.AluOpType
+
+P = 128
+PACK = 4
+BANK = 512
+PASSES = H // (P * PACK)
+SLICES = H // P
+M_TILES = S2 // P
+EARLY = 5
+
+
+def tile_list_ramen_topping_scorer_kernel(
+    tc, tab_words, tab_scales, offs, tab2_words, tab2_scales, offs2, pos1, pos2,
+    w1, w4_words, w4_scales, gain, lunch, base, out,
+):
+    nc = tc.nc
+    with ExitStack() as ctx:
+        lists = ctx.enter_context(tc.tile_pool(name="lists", bufs=1))
+        keep = ctx.enter_context(tc.tile_pool(name="keep", bufs=1))
+        ring = ctx.enter_context(tc.tile_pool(name="ring", bufs=8))
+        psum = ctx.enter_context(tc.psum_pool(name="psum", bufs=1))
+
+        def bank(k, name):
+            return psum.tile([P, BANK], F32, name=name, tag=f"bank{k}")
+
+        idx = lists.tile([P, S // 16], U16, name="idx")
+        idx2 = lists.tile([P, S2 // 16], U16, name="idx2")
+        p1 = lists.tile([P, N // 16], U16, name="p1")
+        p2 = lists.tile([P, N // 16], U16, name="p2")
+
+        v_plane = keep.tile([P, T], U8, name="v_plane", tag="v_plane", align_bytes=64)
+        v2_plane = keep.tile([P, T2], U8, name="v2_plane", tag="v2_plane", align_bytes=64)
+        w4_plane = keep.tile([P, H], U8, name="w4_plane", tag="w4_plane", align_bytes=64)
+        nc.vector.memset(v_plane[:].bitcast(I32), 0)
+        nc.gpsimd.memset(w4_plane[:].bitcast(I32), 0)
+        nc.gpsimd.memset(v2_plane[:].bitcast(I32), 0)
+
+        gain_sb = keep.tile([P, PASSES, PACK], F32, name="gain_sb")
+        lunch_sb = keep.tile([P, PASSES, PACK], F32, name="lunch_sb")
+        w4_raw = keep.tile([P, 2 * H], U8, name="w4_raw", tag="w4_raw", align_bytes=64)
+        v_table = keep.tile([P, T], I32, name="v_table", tag="v_table", align_bytes=64)
+        nc.sync.dma_start(idx[:], offs)
+        nc.sync.dma_start(idx2[:], offs2)
+        nc.sync.dma_start(p1[:], pos1)
+        nc.sync.dma_start(p2[:], pos2)
+        for q in range(4):
+            nc.sync.dma_start(v_plane[32 * q : 32 * q + 4, :].bitcast(I32), tab_scales[0, 4 * q : 4 * q + 4, :].bitcast(I32))
+        nc.sync.dma_start(gain_sb[:], gain.rearrange("(b p t) -> p b t", p=P, t=PACK))
+        nc.sync.dma_start(lunch_sb[:], lunch.rearrange("(b p t) -> p b t", p=P, t=PACK))
+        nc.sync.dma_start(w4_raw[:].bitcast(I32), w4_words[0].bitcast(I32))
+        for q in range(4):
+            nc.sync.dma_start(w4_plane[32 * q : 32 * q + 4, :].bitcast(I32), w4_scales[0, 4 * q : 4 * q + 4, :].bitcast(I32))
+        nc.sync.dma_start(v_table[:], tab_words[0].rearrange("p t i -> p (t i)").bitcast(I32))
+        for q in range(4):
+            nc.sync.dma_start(v2_plane[32 * q : 32 * q + 8, :].bitcast(I32), tab2_scales[:, 4 * q : 4 * q + 4, :].bitcast(I32))
+
+        w1_rows = w1.rearrange("(p j) c -> p j c", j=PACK)
+        w1_raw = {}
+
+        def load_w1(b):
+            for u in range(2):
+                w1_raw[b, u] = keep.tile([P, PACK, 256], F32, name=f"w1_raw{b}{u}", tag=(("v_plane", "w4_raw"), ("w4_plane", "v_table"))[b][u], align_bytes=64)
+                nc.sync.dma_start(w1_raw[b, u][:], w1_rows[:, :, 512 * b + 256 * u : 512 * b + 256 * (u + 1)])
+
+        v2_table = []
+
+        def load_v2_table(a):
+            v2_table.append(keep.tile([P, T2], I32, name=f"v2_table{a}", tag=("v_plane", "v2_plane")[a], align_bytes=64))
+            nc.sync.dma_start(v2_table[a][:], tab2_words[a].rearrange("p t i -> p (t i)").bitcast(I32))
+
+        gain_abs = keep.tile([P, SLICES], F32, name="gain_abs")
+        gain_sign = keep.tile([P, SLICES], F32, name="gain_sign")
+        gain_cols = gain_sb[:].rearrange("p b t -> p (b t)")
+        lunch_cols = lunch_sb[:].rearrange("p b t -> p (b t)")
+        nc.scalar.activation(gain_abs[:], gain_cols, ACT.Abs)
+        nc.scalar.activation(gain_sign[:], gain_cols, ACT.Sign)
+
+        v_scales = keep.tile([P, S], U8, name="v_scales", align_bytes=64)
+        v2_scales = keep.tile([P, S2], U8, name="v2_scales", align_bytes=64)
+        nc.vector.tensor_copy(v_scales[:], v_plane[:].indirect(idx[:]))
+        v_words = keep.tile([P, S], U32, name="v_words", align_bytes=64)
+        for half in range(2):
+            nc.vector.tensor_copy(
+                v_words[:, BANK * half : BANK * (half + 1)],
+                v_table[:].bitcast(U32).indirect(idx[:, 32 * half : 32 * (half + 1)]),
+            )
+
+        w4_codes = keep.tile([P, 2 * H], U8, name="w4_codes", align_bytes=64)
+        w4_sc = keep.tile([P, H], U8, name="w4_sc", align_bytes=64)
+        nc.vector.tensor_copy(
+            w4_codes[:].bitcast(U16).rearrange("p (b t q) -> p b t q", b=PASSES, t=PACK),
+            w4_raw[:].bitcast(U16).rearrange("p (b q t) -> p b t q", b=PASSES, t=PACK),
+        )
+        nc.vector.tensor_copy(
+            w4_sc[:].rearrange("p (b t q) -> p b t q", b=PASSES, t=PACK),
+            w4_plane[:].rearrange("p (b q t) -> p b t q", b=PASSES, t=PACK),
+        )
+
+        w1_codes, w1_scales = [], []
+
+        def quantise_w1(b):
+            grouped = keep.tile([P, PACK, P, PACK], BF16, name=f"w1_grouped{b}", tag=f"w1_grouped{b}", align_bytes=64)
+            for u in range(2):
+                nc.scalar.copy(
+                    grouped[:].rearrange("p t m j -> p m j t")[:, 64 * u : 64 * (u + 1), :, :],
+                    w1_raw[b, u][:].rearrange("p j (m t) -> p m j t", t=PACK),
+                )
+            w1_codes.append(keep.tile([P, BANK], U32, name=f"w1_codes{b}", align_bytes=64))
+            w1_scales.append(keep.tile([P, BANK], U8, name=f"w1_scales{b}", align_bytes=64))
+            nc.vector.quantize_mx(
+                out=w1_codes[b][:].bitcast(FP8X4), scales=w1_scales[b][:],
+                in_=grouped[:].rearrange("p t m j -> p (t m j)"),
+            )
+
+        load_w1(0)
+        nc.vector.tensor_copy(v2_scales[:], v2_plane[:].indirect(idx2[:]))
+        quantise_w1(0)
+        load_w1(1)
+        load_v2_table(0)
+        load_v2_table(1)
+
+        d1_banks, d2_sb, h_sb = {}, {}, {}
+
+        d2_tags = {(0, 0): "w4_raw", (0, 1): "w1_grouped0", (2, 0): "w4_plane", (2, 1): "v_table"}
+
+        def second_features(s):
+            for half in range(2):
+                cols = slice(BANK * half, BANK * (half + 1))
+                d2 = bank(half, f"d2_{s}_{half}")
+                nc.tensor.matmul_mx(
+                    out=d2[:], lhsT=w4_codes[:, 2 * P * s : 2 * P * (s + 1)].bitcast(FP4X4), lhsT_scale=w4_sc[:, P * s : P * (s + 1)],
+                    rhs=v_words[:, cols].bitcast(FP8X4), rhs_scale=v_scales[:, cols], start=True, stop=True,
+                )
+                d2_sb[s, half] = keep.tile([P, BANK], F32, name=f"d2_sb{s}_{half}", tag=d2_tags.get((s, half), f"d2_sb{s}_{half}"), align_bytes=64)
+                nc.scalar.activation(d2_sb[s, half][:], d2[:], ACT.Copy, scale=gain_abs[:, s : s + 1])
+
+        def first_features(s):
+            b, t = divmod(s, PACK)
+            for half in range(2):
+                cols = slice(BANK * half, BANK * (half + 1))
+                d1 = bank(2 + 2 * (s % 3) + half, f"d1_{s}_{half}")
+                nc.tensor.matmul_mx(
+                    out=d1[:], lhsT=w1_codes[b][:, P * t : P * (t + 1)].bitcast(FP8X4), lhsT_scale=w1_scales[b][:, P * t : P * (t + 1)],
+                    rhs=v_words[:, cols].bitcast(FP8X4), rhs_scale=v_scales[:, cols], start=True, stop=True,
+                )
+                d1_banks[s, half] = d1
+
+        def first_maximum(s):
+            h_sb[s] = keep.tile([P, S], F32, name=f"h_sb{s}")
+            for half in range(2):
+                cols = slice(BANK * half, BANK * (half + 1))
+                nc.vector.scalar_tensor_tensor(
+                    out=h_sb[s][:, cols], in0=d1_banks[s, half][:], scalar=gain_abs[:, s : s + 1],
+                    in1=d2_sb[s, half][:], op0=ALU.mult, op1=ALU.max,
+                )
+
+        x1_planes = [keep.tile([P, PACK, N], BF16, name=f"x1_planes{b}", tag=f"x1_planes{b}", align_bytes=64) for b in range(PASSES)]
+
+        def pick_lunch(s):
+            b, t = divmod(s, PACK)
+            picked = ring.tile([P, N], F32, name="picked")
+            nc.vector.tensor_copy(picked[:], h_sb[s][:].indirect(p1[:]))
+            nc.scalar.activation(
+                x1_planes[b][:, t, :], picked[:], ACT.Identity, scale=gain_sign[:, s : s + 1], bias=lunch_cols[:, s : s + 1],
+            )
+
+        x_codes = {(x, b): keep.tile([P, N], U32, name=f"x{x}_codes{b}", align_bytes=64) for x in (1, 2) for b in range(PASSES)}
+        x_scales = {(x, b): keep.tile([P, N], U8, name=f"x{x}_scales{b}", align_bytes=64) for x in (1, 2) for b in range(PASSES)}
+
+        def quantise_x(x, b, woven, cols):
+            nc.vector.quantize_mx(
+                out=x_codes[x, b][:, cols].bitcast(FP8X4), scales=x_scales[x, b][:, cols],
+                in_=woven[:].rearrange("p n t -> p (n t)"),
+            )
+
+        def weave_lunch(b):
+            woven = keep.tile([P, N, PACK], BF16, name=f"x1_woven{b}", tag=f"x1_woven{b}", align_bytes=64)
+            nc.scalar.copy(
+                woven[:].rearrange("p (c i) t -> p c t i", i=4),
+                x1_planes[b][:].rearrange("p t (c i) -> p c t i", i=4),
+            )
+            quantise_x(1, b, woven, slice(0, N))
+
+        def weave_evening(b, picked, cols, tag):
+            width = cols.stop - cols.start
+            woven = keep.tile([P, width, PACK], BF16, name=f"x2_woven{b}_{cols.start}", tag=tag, align_bytes=64)
+            nc.scalar.activation(
+                woven[:].rearrange("p (c i) t -> p c t i", i=4),
+                picked.rearrange("p t (c i) -> p c t i", i=4),
+                ACT.Abs,
+            )
+            quantise_x(2, b, woven, cols)
+
+        v2_words = {}
+
+        def pick_toppings(a, m0, m1, tag):
+            words = keep.tile([P, P * (m1 - m0)], U32, name=f"v2_words{a}_{m0}", tag=tag, align_bytes=64)
+            nc.vector.tensor_copy(words[:], v2_table[a][:].bitcast(U32).indirect(idx2[:, 8 * m0 : 8 * m1]))
+            for m in range(m0, m1):
+                v2_words[a, m] = words[:, P * (m - m0) : P * (m - m0 + 1)]
+
+        evening0 = keep.tile([P, PACK, N], F32, name="evening0")
+
+        for s in range(SLICES):
+            if s < 3:
+                first_features(s)
+            second_features(s)
+            if s == 1:
+                quantise_w1(1)
+        for s in range(SLICES):
+            first_maximum(s)
+            if s + 3 < SLICES:
+                first_features(s + 3)
+            pick_lunch(s)
+            if s < PACK:
+                nc.vector.tensor_copy(evening0[:, s, :], h_sb[s][:].indirect(p2[:]))
+            if s < PASSES:
+                pick_toppings(s, 0, EARLY, f"v2_early{s}")
+            if s == PACK - 1:
+                weave_lunch(0)
+            if s == PACK:
+                weave_evening(0, evening0[:], slice(0, N), "x2_woven0")
+
+        base_sb = keep.tile([P, M_TILES], F32, name="base_sb", tag="w4_raw", align_bytes=64)
+        with nc.allow_non_contiguous_dma(reason="one base value to a partition"):
+            nc.sync.dma_start(base_sb[:], base.rearrange("(c p) -> p c", p=P))
+
+        last = SLICES - 1
+
+        def pick_evening(half, tag):
+            picked = keep.tile([P, PACK, N // 2], F32, name=f"evening1_{half}", tag=tag, align_bytes=64)
+            for t in range(PACK):
+                nc.vector.tensor_copy(picked[:, t, :], h_sb[PACK + t][:].indirect(p2[:, 16 * half : 16 * (half + 1)]))
+            return picked
+
+        def second_pass(acc, x, b, m, cols, start, stop):
+            nc.tensor.matmul_mx(
+                out=acc[:, cols], lhsT=v2_words[b, m].bitcast(FP8X4),
+                lhsT_scale=v2_scales[4 * b : P, P * m : P * (m + 1)],
+                rhs=x_codes[x, b][:, cols].bitcast(FP8X4), rhs_scale=x_scales[x, b][:, cols], start=start, stop=stop,
+            )
+
+        e1_sb = []
+        e_banks = (0, 1, 6, 7, 2, 3, 4, 5)
+
+        def lunch_scores(m):
+            e1 = bank(e_banks[m], f"e1_{m}")
+            for b in range(PASSES):
+                second_pass(e1, 1, b, m, slice(0, N), b == 0, b == PASSES - 1)
+            e1_sb.append(keep.tile([P, N], F32, name=f"e1_sb{m}"))
+            nc.scalar.activation(e1_sb[m][:], e1[:], ACT.Identity, bias=base_sb[:, m : m + 1])
+
+        first_half = pick_evening(0, f"d2_sb{last}_0")
+        pick_toppings(0, EARLY, M_TILES, f"d2_sb{last}_1")
+        weave_lunch(1)
+        weave_evening(1, first_half[:], slice(0, 256), "x1_planes1")
+        second_half = pick_evening(1, "x1_woven1")
+        pick_toppings(1, EARLY, M_TILES, f"d2_sb{last}_0")
+        e2_banks = {}
+
+        def open_evening_scores(m):
+            e2_banks[m] = bank(e_banks[m], f"e2_{m}")
+            second_pass(e2_banks[m], 2, 0, m, slice(0, N), True, False)
+            second_pass(e2_banks[m], 2, 1, m, slice(0, 256), False, False)
+
+        def close_evening_scores(m):
+            second_pass(e2_banks[m], 2, 1, m, slice(256, N), False, True)
+            result = keep.tile([P, N], F32, name=f"result{m}")
+            nc.vector.scalar_tensor_tensor(
+                out=result[:], in0=e2_banks[m][:], scalar=base_sb[:, m : m + 1], in1=e1_sb[m][:], op0=ALU.add, op1=ALU.max,
+            )
+            nc.sync.dma_start(out[P * m : P * (m + 1), :], result[:])
+
+        for m in range(3):
+            lunch_scores(m)
+            open_evening_scores(m)
+        weave_evening(1, second_half[:], slice(256, N), "x2_woven1")
+        for m in range(3, EARLY):
+            lunch_scores(m)
+            open_evening_scores(m)
+        for m in range(M_TILES):
+            if EARLY <= m + 3 < M_TILES:
+                lunch_scores(m + 3)
+                open_evening_scores(m + 3)
+            close_evening_scores(m)

@@ -47,28 +47,29 @@ def tile_list_ramen_topping_scorer_kernel(
         v_plane = keep.tile([P, T], U8, name="v_plane", tag="v_plane", align_bytes=64)
         v2_plane = keep.tile([P, T2], U8, name="v2_plane", tag="v2_plane", align_bytes=64)
         w4_plane = keep.tile([P, H], U8, name="w4_plane", tag="w4_plane", align_bytes=64)
+        v_scales = keep.tile([P, S], U8, name="v_scales", align_bytes=64)
         nc.vector.memset(v_plane[:].bitcast(I32), 0)
         nc.gpsimd.memset(w4_plane[:].bitcast(I32), 0)
         nc.gpsimd.memset(v2_plane[:].bitcast(I32), 0)
+        nc.vector.memset(v_scales[:].bitcast(I32), 0)
 
         gain_sb = keep.tile([P, PASSES, PACK], F32, name="gain_sb")
         lunch_sb = keep.tile([P, PASSES, PACK], F32, name="lunch_sb")
         w4_raw = keep.tile([P, 2 * H], U8, name="w4_raw", tag="w4_raw", align_bytes=64)
         v_table = keep.tile([P, T], I32, name="v_table", tag="v_table", align_bytes=64)
         nc.sync.dma_start(idx[:], offs)
-        nc.sync.dma_start(idx2[:], offs2)
-        nc.sync.dma_start(p1[:], pos1)
-        nc.sync.dma_start(p2[:], pos2)
-        for q in range(4):
-            nc.sync.dma_start(v_plane[32 * q : 32 * q + 4, :].bitcast(I32), tab_scales[0, 4 * q : 4 * q + 4, :].bitcast(I32))
-        nc.sync.dma_start(gain_sb[:], gain.rearrange("(b p t) -> p b t", p=P, t=PACK))
-        nc.sync.dma_start(lunch_sb[:], lunch.rearrange("(b p t) -> p b t", p=P, t=PACK))
+        nc.sync.dma_start(v_plane[0:16, :].bitcast(I32), tab_scales[0].bitcast(I32))
+        nc.scalar.dma_start(v_table[:], tab_words[0].rearrange("p t i -> p (t i)").bitcast(I32))
         nc.sync.dma_start(w4_raw[:].bitcast(I32), w4_words[0].bitcast(I32))
         for q in range(4):
             nc.sync.dma_start(w4_plane[32 * q : 32 * q + 4, :].bitcast(I32), w4_scales[0, 4 * q : 4 * q + 4, :].bitcast(I32))
-        nc.sync.dma_start(v_table[:], tab_words[0].rearrange("p t i -> p (t i)").bitcast(I32))
+        nc.sync.dma_start(idx2[:], offs2)
+        nc.sync.dma_start(p1[:], pos1)
+        nc.sync.dma_start(p2[:], pos2)
+        nc.gpsimd.dma_start(gain_sb[:], gain.rearrange("(b p t) -> p b t", p=P, t=PACK))
         for q in range(4):
-            nc.sync.dma_start(v2_plane[32 * q : 32 * q + 8, :].bitcast(I32), tab2_scales[:, 4 * q : 4 * q + 4, :].bitcast(I32))
+            nc.gpsimd.dma_start(v2_plane[32 * q : 32 * q + 8, :].bitcast(I32), tab2_scales[:, 4 * q : 4 * q + 4, :].bitcast(I32))
+        nc.gpsimd.dma_start(lunch_sb[:], lunch.rearrange("(b p t) -> p b t", p=P, t=PACK))
 
         w1_rows = w1.rearrange("(p j) c -> p j c", j=PACK)
         w1_raw = {}
@@ -91,9 +92,11 @@ def tile_list_ramen_topping_scorer_kernel(
         nc.scalar.activation(gain_abs[:], gain_cols, ACT.Abs)
         nc.scalar.activation(gain_sign[:], gain_cols, ACT.Sign)
 
-        v_scales = keep.tile([P, S], U8, name="v_scales", align_bytes=64)
+        v_rows = keep.tile([P, S], U8, name="v_rows", align_bytes=64)
         v2_scales = keep.tile([P, S2], U8, name="v2_scales", align_bytes=64)
-        nc.vector.tensor_copy(v_scales[:], v_plane[:].indirect(idx[:]))
+        nc.vector.tensor_copy(v_rows[:], v_plane[:].indirect(idx[:]))
+        for q in range(4):
+            nc.sync.dma_start(v_scales[32 * q : 32 * q + 4, :].bitcast(I32), v_rows[4 * q : 4 * q + 4, :].bitcast(I32))
         v_words = keep.tile([P, S], U32, name="v_words", align_bytes=64)
         for half in range(2):
             nc.vector.tensor_copy(
@@ -104,12 +107,12 @@ def tile_list_ramen_topping_scorer_kernel(
         w4_codes = keep.tile([P, 2 * H], U8, name="w4_codes", align_bytes=64)
         w4_sc = keep.tile([P, H], U8, name="w4_sc", align_bytes=64)
         nc.vector.tensor_copy(
-            w4_codes[:].bitcast(U16).rearrange("p (b t q) -> p b t q", b=PASSES, t=PACK),
-            w4_raw[:].bitcast(U16).rearrange("p (b q t) -> p b t q", b=PASSES, t=PACK),
+            w4_codes[:].bitcast(U16).rearrange("p (b t q) -> p b q t", b=PASSES, t=PACK),
+            w4_raw[:].bitcast(U16).rearrange("p (b q t) -> p b q t", b=PASSES, t=PACK),
         )
         nc.vector.tensor_copy(
-            w4_sc[:].rearrange("p (b t q) -> p b t q", b=PASSES, t=PACK),
-            w4_plane[:].rearrange("p (b q t) -> p b t q", b=PASSES, t=PACK),
+            w4_sc[:].rearrange("p (b t q) -> p b q t", b=PASSES, t=PACK),
+            w4_plane[:].rearrange("p (b q t) -> p b q t", b=PASSES, t=PACK),
         )
 
         w1_codes, w1_scales = [], []
@@ -215,8 +218,6 @@ def tile_list_ramen_topping_scorer_kernel(
             for m in range(m0, m1):
                 v2_words[a, m] = words[:, P * (m - m0) : P * (m - m0 + 1)]
 
-        evening0 = keep.tile([P, PACK, N], F32, name="evening0")
-
         for s in range(SLICES):
             if s < 3:
                 first_features(s)
@@ -228,26 +229,18 @@ def tile_list_ramen_topping_scorer_kernel(
             if s + 3 < SLICES:
                 first_features(s + 3)
             pick_lunch(s)
-            if s < PACK:
-                nc.vector.tensor_copy(evening0[:, s, :], h_sb[s][:].indirect(p2[:]))
-            if s < PASSES:
-                pick_toppings(s, 0, EARLY, f"v2_early{s}")
+            if s == 0:
+                pick_toppings(0, 0, M_TILES, "v2_words0")
+            if s == 1:
+                pick_toppings(1, 0, EARLY, "v2_words1")
             if s == PACK - 1:
                 weave_lunch(0)
-            if s == PACK:
-                weave_evening(0, evening0[:], slice(0, N), "x2_woven0")
 
         base_sb = keep.tile([P, M_TILES], F32, name="base_sb", tag="w4_raw", align_bytes=64)
         with nc.allow_non_contiguous_dma(reason="one base value to a partition"):
             nc.sync.dma_start(base_sb[:], base.rearrange("(c p) -> p c", p=P))
 
         last = SLICES - 1
-
-        def pick_evening(half, tag):
-            picked = keep.tile([P, PACK, N // 2], F32, name=f"evening1_{half}", tag=tag, align_bytes=64)
-            for t in range(PACK):
-                nc.vector.tensor_copy(picked[:, t, :], h_sb[PACK + t][:].indirect(p2[:, 16 * half : 16 * (half + 1)]))
-            return picked
 
         def second_pass(acc, x, b, m, cols, start, stop):
             nc.tensor.matmul_mx(
@@ -266,12 +259,6 @@ def tile_list_ramen_topping_scorer_kernel(
             e1_sb.append(keep.tile([P, N], F32, name=f"e1_sb{m}"))
             nc.scalar.activation(e1_sb[m][:], e1[:], ACT.Identity, bias=base_sb[:, m : m + 1])
 
-        first_half = pick_evening(0, f"d2_sb{last}_0")
-        pick_toppings(0, EARLY, M_TILES, f"d2_sb{last}_1")
-        weave_lunch(1)
-        weave_evening(1, first_half[:], slice(0, 256), "x1_planes1")
-        second_half = pick_evening(1, "x1_woven1")
-        pick_toppings(1, EARLY, M_TILES, f"d2_sb{last}_0")
         e2_banks = {}
 
         def open_evening_scores(m):
@@ -287,11 +274,23 @@ def tile_list_ramen_topping_scorer_kernel(
             )
             nc.sync.dma_start(out[P * m : P * (m + 1), :], result[:])
 
-        for m in range(3):
-            lunch_scores(m)
-            open_evening_scores(m)
-        weave_evening(1, second_half[:], slice(256, N), "x2_woven1")
-        for m in range(3, EARLY):
+        evening0 = keep.tile([P, PACK, N], F32, name="evening0", tag=f"d2_sb{last}_0", align_bytes=64)
+        for t in range(PACK):
+            nc.vector.tensor_copy(evening0[:, t, :], h_sb[t][:].indirect(p2[:]))
+        weave_lunch(1)
+        weave_evening(0, evening0[:], slice(0, N), "x1_planes1")
+        evening1 = keep.tile([P, 2, PACK, N // 2], F32, name="evening1", tag="x1_woven1", align_bytes=64)
+        for half in range(2):
+            for t in range(PACK):
+                nc.vector.tensor_copy(evening1[:, half, t, :], h_sb[PACK + t][:].indirect(p2[:, 16 * half : 16 * (half + 1)]))
+        lunch_scores(0)
+        weave_evening(1, evening1[:, 0, :, :], slice(0, 256), "x2_woven1_0")
+        pick_toppings(1, EARLY, M_TILES, "x2_woven1_0")
+        open_evening_scores(0)
+        lunch_scores(1)
+        open_evening_scores(1)
+        weave_evening(1, evening1[:, 1, :, :], slice(256, N), "x2_woven1_1")
+        for m in range(2, EARLY):
             lunch_scores(m)
             open_evening_scores(m)
         for m in range(M_TILES):

@@ -48,36 +48,37 @@ def tile_list_ramen_topping_scorer_kernel(
         v2_plane = keep.tile([P, T2], U8, name="v2_plane", tag="v2_plane", align_bytes=64)
         w4_plane = keep.tile([P, H], U8, name="w4_plane", tag="w4_plane", align_bytes=64)
         v_scales = keep.tile([P, S], U8, name="v_scales", align_bytes=64)
-        nc.vector.memset(v_plane[:].bitcast(I32), 0)
         nc.gpsimd.memset(w4_plane[:].bitcast(I32), 0)
-        nc.gpsimd.memset(v2_plane[:].bitcast(I32), 0)
+        nc.vector.memset(v2_plane[:].bitcast(I32), 0)
+        nc.vector.memset(v_plane[0:112, :].bitcast(I32), 0)
         nc.vector.memset(v_scales[:].bitcast(I32), 0)
 
         gain_sb = keep.tile([P, PASSES, PACK], F32, name="gain_sb")
         lunch_sb = keep.tile([P, PASSES, PACK], F32, name="lunch_sb")
         w4_raw = keep.tile([P, 2 * H], U8, name="w4_raw", tag="w4_raw", align_bytes=64)
         v_table = keep.tile([P, T], I32, name="v_table", tag="v_table", align_bytes=64)
-        nc.sync.dma_start(idx[:], offs)
-        nc.sync.dma_start(v_plane[0:16, :].bitcast(I32), tab_scales[0].bitcast(I32))
-        nc.scalar.dma_start(v_table[:], tab_words[0].rearrange("p t i -> p (t i)").bitcast(I32))
-        nc.sync.dma_start(w4_raw[:].bitcast(I32), w4_words[0].bitcast(I32))
-        for q in range(4):
-            nc.sync.dma_start(w4_plane[32 * q : 32 * q + 4, :].bitcast(I32), w4_scales[0, 4 * q : 4 * q + 4, :].bitcast(I32))
-        nc.sync.dma_start(idx2[:], offs2)
-        nc.sync.dma_start(p1[:], pos1)
-        nc.sync.dma_start(p2[:], pos2)
-        nc.gpsimd.dma_start(gain_sb[:], gain.rearrange("(b p t) -> p b t", p=P, t=PACK))
-        for q in range(4):
-            nc.gpsimd.dma_start(v2_plane[32 * q : 32 * q + 8, :].bitcast(I32), tab2_scales[:, 4 * q : 4 * q + 4, :].bitcast(I32))
-        nc.gpsimd.dma_start(lunch_sb[:], lunch.rearrange("(b p t) -> p b t", p=P, t=PACK))
-
         w1_rows = w1.rearrange("(p j) c -> p j c", j=PACK)
         w1_raw = {}
 
         def load_w1(b):
             for u in range(2):
-                w1_raw[b, u] = keep.tile([P, PACK, 256], F32, name=f"w1_raw{b}{u}", tag=(("v_plane", "w4_raw"), ("w4_plane", "v_table"))[b][u], align_bytes=64)
+                w1_raw[b, u] = keep.tile([P, PACK, 256], F32, name=f"w1_raw{b}{u}", tag=(("w1_raw00", "w1_raw01"), ("w1_raw00", "v_table"))[b][u], align_bytes=64)
                 nc.sync.dma_start(w1_raw[b, u][:], w1_rows[:, :, 512 * b + 256 * u : 512 * b + 256 * (u + 1)])
+
+        nc.sync.dma_start(idx[:], offs)
+        nc.sync.dma_start(v_plane[112:P, :].bitcast(I32), tab_scales[0].bitcast(I32))
+        nc.sync.dma_start(w4_raw[:].bitcast(I32), w4_words[0].bitcast(I32))
+        nc.sync.dma_start(gain_sb[:], gain.rearrange("(b p t) -> p b t", p=P, t=PACK))
+        nc.sync.dma_start(idx2[:], offs2)
+        nc.sync.dma_start(v_table[:], tab_words[0].rearrange("p t i -> p (t i)").bitcast(I32))
+        load_w1(0)
+        nc.sync.dma_start(p1[:], pos1)
+        nc.sync.dma_start(p2[:], pos2)
+        for q in range(4):
+            nc.sync.dma_start(v2_plane[32 * q : 32 * q + 8, :].bitcast(I32), tab2_scales[:, 4 * q : 4 * q + 4, :].bitcast(I32))
+        for q in range(4):
+            nc.gpsimd.dma_start(w4_plane[32 * q : 32 * q + 4, :].bitcast(I32), w4_scales[0, 4 * q : 4 * q + 4, :].bitcast(I32))
+        nc.gpsimd.dma_start(lunch_sb[:], lunch.rearrange("(b p t) -> p b t", p=P, t=PACK))
 
         v2_table = []
 
@@ -96,7 +97,7 @@ def tile_list_ramen_topping_scorer_kernel(
         v2_scales = keep.tile([P, S2], U8, name="v2_scales", align_bytes=64)
         nc.vector.tensor_copy(v_rows[:], v_plane[:].indirect(idx[:]))
         for q in range(4):
-            nc.sync.dma_start(v_scales[32 * q : 32 * q + 4, :].bitcast(I32), v_rows[4 * q : 4 * q + 4, :].bitcast(I32))
+            nc.sync.dma_start(v_scales[32 * q : 32 * q + 4, :].bitcast(I32), v_rows[112 + 4 * q : 116 + 4 * q, :].bitcast(I32))
         v_words = keep.tile([P, S], U32, name="v_words", align_bytes=64)
         for half in range(2):
             nc.vector.tensor_copy(
@@ -117,22 +118,27 @@ def tile_list_ramen_topping_scorer_kernel(
 
         w1_codes, w1_scales = [], []
 
-        def quantise_w1(b):
-            grouped = keep.tile([P, PACK, P, PACK], BF16, name=f"w1_grouped{b}", tag=f"w1_grouped{b}", align_bytes=64)
+        w1_grouped = []
+
+        def cast_w1(b):
+            grouped = keep.tile([P, PACK, P, PACK], BF16, name=f"w1_grouped{b}", tag=("w1_grouped0", "w1_raw01")[b], align_bytes=64)
             for u in range(2):
                 nc.scalar.copy(
                     grouped[:].rearrange("p t m j -> p m j t")[:, 64 * u : 64 * (u + 1), :, :],
                     w1_raw[b, u][:].rearrange("p j (m t) -> p m j t", t=PACK),
                 )
-            w1_codes.append(keep.tile([P, BANK], U32, name=f"w1_codes{b}", align_bytes=64))
+            w1_grouped.append(grouped)
+
+        def quantise_w1(b):
+            w1_codes.append(keep.tile([P, BANK], U32, name=f"w1_codes{b}", tag=("w1_codes0", "d2_sb1_1")[b], align_bytes=64))
             w1_scales.append(keep.tile([P, BANK], U8, name=f"w1_scales{b}", align_bytes=64))
             nc.vector.quantize_mx(
                 out=w1_codes[b][:].bitcast(FP8X4), scales=w1_scales[b][:],
-                in_=grouped[:].rearrange("p t m j -> p (t m j)"),
+                in_=w1_grouped[b][:].rearrange("p t m j -> p (t m j)"),
             )
 
-        load_w1(0)
         nc.vector.tensor_copy(v2_scales[:], v2_plane[:].indirect(idx2[:]))
+        cast_w1(0)
         quantise_w1(0)
         load_w1(1)
         load_v2_table(0)
@@ -140,7 +146,7 @@ def tile_list_ramen_topping_scorer_kernel(
 
         d1_banks, d2_sb, h_sb = {}, {}, {}
 
-        d2_tags = {(0, 0): "w4_raw", (0, 1): "w1_grouped0", (2, 0): "w4_plane", (2, 1): "v_table"}
+        d2_tags = {(0, 0): "w1_raw01", (0, 1): "w1_grouped0", (2, 0): "w1_raw00", (2, 1): "v_table"}
 
         def second_features(s):
             for half in range(2):
@@ -200,15 +206,18 @@ def tile_list_ramen_topping_scorer_kernel(
             )
             quantise_x(1, b, woven, slice(0, N))
 
-        def weave_evening(b, picked, cols, tag):
-            width = cols.stop - cols.start
-            woven = keep.tile([P, width, PACK], BF16, name=f"x2_woven{b}_{cols.start}", tag=tag, align_bytes=64)
+        def pick_evening(b, half, tag):
+            picked = keep.tile([P, PACK, N // 2], F32, name=f"evening{b}_{half}", tag=tag, align_bytes=64)
+            for t in range(PACK):
+                nc.vector.tensor_copy(picked[:, t, :], h_sb[PACK * b + t][:].indirect(p2[:, 16 * half : 16 * (half + 1)]))
+            return picked
+
+        def weave_evening(woven, picked):
             nc.scalar.activation(
-                woven[:].rearrange("p (c i) t -> p c t i", i=4),
-                picked.rearrange("p t (c i) -> p c t i", i=4),
+                woven.rearrange("p (c i) t -> p c t i", i=4),
+                picked[:].rearrange("p t (c i) -> p c t i", i=4),
                 ACT.Abs,
             )
-            quantise_x(2, b, woven, cols)
 
         v2_words = {}
 
@@ -218,25 +227,29 @@ def tile_list_ramen_topping_scorer_kernel(
             for m in range(m0, m1):
                 v2_words[a, m] = words[:, P * (m - m0) : P * (m - m0 + 1)]
 
-        for s in range(SLICES):
-            if s < 3:
-                first_features(s)
+        for s in range(2):
             second_features(s)
+            first_features(s)
+        first_features(2)
+        first_maximum(0)
+        cast_w1(1)
+        for s in range(2, SLICES):
+            second_features(s)
+        for s in range(SLICES):
+            if s > 0:
+                first_maximum(s)
             if s == 1:
                 quantise_w1(1)
-        for s in range(SLICES):
-            first_maximum(s)
             if s + 3 < SLICES:
                 first_features(s + 3)
             pick_lunch(s)
             if s == 0:
-                pick_toppings(0, 0, M_TILES, "v2_words0")
-            if s == 1:
-                pick_toppings(1, 0, EARLY, "v2_words1")
+                pick_toppings(0, 0, EARLY, "v2_words0")
             if s == PACK - 1:
+                pick_toppings(1, 0, EARLY, "d2_sb3_0")
                 weave_lunch(0)
 
-        base_sb = keep.tile([P, M_TILES], F32, name="base_sb", tag="w4_raw", align_bytes=64)
+        base_sb = keep.tile([P, M_TILES], F32, name="base_sb", tag="d2_sb1_0", align_bytes=64)
         with nc.allow_non_contiguous_dma(reason="one base value to a partition"):
             nc.sync.dma_start(base_sb[:], base.rearrange("(c p) -> p c", p=P))
 
@@ -274,25 +287,28 @@ def tile_list_ramen_topping_scorer_kernel(
             )
             nc.sync.dma_start(out[P * m : P * (m + 1), :], result[:])
 
-        evening0 = keep.tile([P, PACK, N], F32, name="evening0", tag=f"d2_sb{last}_0", align_bytes=64)
-        for t in range(PACK):
-            nc.vector.tensor_copy(evening0[:, t, :], h_sb[t][:].indirect(p2[:]))
+        picked = pick_evening(0, 0, f"d2_sb{last}_0")
+        pick_toppings(0, EARLY, M_TILES, f"d2_sb{last}_1")
         weave_lunch(1)
-        weave_evening(0, evening0[:], slice(0, N), "x1_planes1")
-        evening1 = keep.tile([P, 2, PACK, N // 2], F32, name="evening1", tag="x1_woven1", align_bytes=64)
-        for half in range(2):
-            for t in range(PACK):
-                nc.vector.tensor_copy(evening1[:, half, t, :], h_sb[PACK + t][:].indirect(p2[:, 16 * half : 16 * (half + 1)]))
-        lunch_scores(0)
-        weave_evening(1, evening1[:, 0, :, :], slice(0, 256), "x2_woven1_0")
-        pick_toppings(1, EARLY, M_TILES, "x2_woven1_0")
-        open_evening_scores(0)
-        lunch_scores(1)
-        open_evening_scores(1)
-        weave_evening(1, evening1[:, 1, :, :], slice(256, N), "x2_woven1_1")
-        for m in range(2, EARLY):
+        woven0 = keep.tile([P, N, PACK], BF16, name="x2_woven0", tag="x1_planes1", align_bytes=64)
+        weave_evening(woven0[:, 0:256, :], picked)
+        picked = pick_evening(0, 1, "x1_woven1")
+        for m in range(3):
             lunch_scores(m)
+        weave_evening(woven0[:, 256:N, :], picked)
+        picked = pick_evening(1, 0, f"d2_sb{last}_0")
+        quantise_x(2, 0, woven0, slice(0, N))
+        for m in range(3, EARLY):
+            lunch_scores(m)
+        woven1 = [keep.tile([P, N // 2, PACK], BF16, name=f"x2_woven1_{half}", tag=f"x2_woven1_{half}", align_bytes=64) for half in range(2)]
+        weave_evening(woven1[0][:], picked)
+        picked = pick_evening(1, 1, "x1_planes1")
+        quantise_x(2, 1, woven1[0], slice(0, 256))
+        pick_toppings(1, EARLY, M_TILES, "x2_woven1_0")
+        for m in range(EARLY):
             open_evening_scores(m)
+        weave_evening(woven1[1][:], picked)
+        quantise_x(2, 1, woven1[1], slice(256, N))
         for m in range(M_TILES):
             if EARLY <= m + 3 < M_TILES:
                 lunch_scores(m + 3)

@@ -33,7 +33,6 @@ def tile_list_ramen_topping_scorer_kernel(
     with ExitStack() as ctx:
         lists = ctx.enter_context(tc.tile_pool(name="lists", bufs=1))
         keep = ctx.enter_context(tc.tile_pool(name="keep", bufs=1))
-        ring = ctx.enter_context(tc.tile_pool(name="ring", bufs=8))
         psum = ctx.enter_context(tc.psum_pool(name="psum", bufs=1))
 
         def bank(k, name):
@@ -94,7 +93,6 @@ def tile_list_ramen_topping_scorer_kernel(
         nc.scalar.activation(gain_sign[:], gain_cols, ACT.Sign)
 
         v_rows = keep.tile([P, S], U8, name="v_rows", align_bytes=64)
-        v2_scales = keep.tile([P, S2], U8, name="v2_scales", align_bytes=64)
         nc.vector.tensor_copy(v_rows[:], v_plane[:].indirect(idx[:]))
         for q in range(4):
             nc.sync.dma_start(v_scales[32 * q : 32 * q + 4, :].bitcast(I32), v_rows[112 + 4 * q : 116 + 4 * q, :].bitcast(I32))
@@ -130,25 +128,31 @@ def tile_list_ramen_topping_scorer_kernel(
             w1_grouped.append(grouped)
 
         def quantise_w1(b):
-            w1_codes.append(keep.tile([P, BANK], U32, name=f"w1_codes{b}", tag=("w1_codes0", "d2_sb1_1")[b], align_bytes=64))
+            w1_codes.append(keep.tile([P, BANK], U32, name=f"w1_codes{b}", tag=("w1_codes0", "d2_sb2")[b], align_bytes=64))
             w1_scales.append(keep.tile([P, BANK], U8, name=f"w1_scales{b}", align_bytes=64))
             nc.vector.quantize_mx(
                 out=w1_codes[b][:].bitcast(FP8X4), scales=w1_scales[b][:],
                 in_=w1_grouped[b][:].rearrange("p t m j -> p (t m j)"),
             )
 
-        nc.vector.tensor_copy(v2_scales[:], v2_plane[:].indirect(idx2[:]))
+        v2_scales = []
+
+        def pick_v2_scales(half):
+            v2_scales.append(keep.tile([P, S2 // 2], U8, name=f"v2_scales{half}", tag=("v2_scales0", "w1_grouped0")[half], align_bytes=64))
+            nc.vector.tensor_copy(v2_scales[half][:], v2_plane[:].indirect(idx2[:, 32 * half : 32 * (half + 1)]))
+
+        pick_v2_scales(0)
         cast_w1(0)
         quantise_w1(0)
-        load_w1(1)
+        pick_v2_scales(1)
         load_v2_table(0)
+        load_w1(1)
         load_v2_table(1)
 
         d1_banks, d2_sb, h_sb = {}, {}, {}
 
-        d2_tags = {(0, 0): "w1_raw01", (0, 1): "w1_grouped0", (2, 0): "w1_raw00", (2, 1): "v_table"}
-
         def second_features(s):
+            d2_sb[s] = keep.tile([P, S], F32, name=f"d2_sb{s}", tag=f"d2_sb{s}" if s else "w1_raw01", align_bytes=64)
             for half in range(2):
                 cols = slice(BANK * half, BANK * (half + 1))
                 d2 = bank(half, f"d2_{s}_{half}")
@@ -156,8 +160,7 @@ def tile_list_ramen_topping_scorer_kernel(
                     out=d2[:], lhsT=w4_codes[:, 2 * P * s : 2 * P * (s + 1)].bitcast(FP4X4), lhsT_scale=w4_sc[:, P * s : P * (s + 1)],
                     rhs=v_words[:, cols].bitcast(FP8X4), rhs_scale=v_scales[:, cols], start=True, stop=True,
                 )
-                d2_sb[s, half] = keep.tile([P, BANK], F32, name=f"d2_sb{s}_{half}", tag=d2_tags.get((s, half), f"d2_sb{s}_{half}"), align_bytes=64)
-                nc.scalar.activation(d2_sb[s, half][:], d2[:], ACT.Copy, scale=gain_abs[:, s : s + 1])
+                nc.scalar.activation(d2_sb[s][:, cols], d2[:], ACT.Copy, scale=gain_abs[:, s : s + 1])
 
         def first_features(s):
             b, t = divmod(s, PACK)
@@ -176,14 +179,14 @@ def tile_list_ramen_topping_scorer_kernel(
                 cols = slice(BANK * half, BANK * (half + 1))
                 nc.vector.scalar_tensor_tensor(
                     out=h_sb[s][:, cols], in0=d1_banks[s, half][:], scalar=gain_abs[:, s : s + 1],
-                    in1=d2_sb[s, half][:], op0=ALU.mult, op1=ALU.max,
+                    in1=d2_sb[s][:, cols], op0=ALU.mult, op1=ALU.max,
                 )
 
         x1_planes = [keep.tile([P, PACK, N], BF16, name=f"x1_planes{b}", tag=f"x1_planes{b}", align_bytes=64) for b in range(PASSES)]
 
         def pick_lunch(s):
             b, t = divmod(s, PACK)
-            picked = ring.tile([P, N], F32, name="picked")
+            picked = keep.tile([P, N], F32, name=f"picked{s}", tag=f"picked{s}", align_bytes=64)
             nc.vector.tensor_copy(picked[:], h_sb[s][:].indirect(p1[:]))
             nc.scalar.activation(
                 x1_planes[b][:, t, :], picked[:], ACT.Identity, scale=gain_sign[:, s : s + 1], bias=lunch_cols[:, s : s + 1],
@@ -238,18 +241,21 @@ def tile_list_ramen_topping_scorer_kernel(
         for s in range(SLICES):
             if s > 0:
                 first_maximum(s)
-            if s == 1:
+            if s == 0:
+                first_features(3)
+            if s == 2:
                 quantise_w1(1)
-            if s + 3 < SLICES:
+                first_features(4)
+            if 2 <= s < SLICES - 3:
                 first_features(s + 3)
             pick_lunch(s)
-            if s == 0:
-                pick_toppings(0, 0, EARLY, "v2_words0")
+            if s == 1:
+                pick_toppings(0, 0, EARLY, "d2_sb1")
             if s == PACK - 1:
-                pick_toppings(1, 0, EARLY, "d2_sb3_0")
+                pick_toppings(1, 0, EARLY, "d2_sb3")
                 weave_lunch(0)
 
-        base_sb = keep.tile([P, M_TILES], F32, name="base_sb", tag="d2_sb1_0", align_bytes=64)
+        base_sb = keep.tile([P, M_TILES], F32, name="base_sb", tag="d2_sb4", align_bytes=64)
         with nc.allow_non_contiguous_dma(reason="one base value to a partition"):
             nc.sync.dma_start(base_sb[:], base.rearrange("(c p) -> p c", p=P))
 
@@ -258,7 +264,7 @@ def tile_list_ramen_topping_scorer_kernel(
         def second_pass(acc, x, b, m, cols, start, stop):
             nc.tensor.matmul_mx(
                 out=acc[:, cols], lhsT=v2_words[b, m].bitcast(FP8X4),
-                lhsT_scale=v2_scales[4 * b : P, P * m : P * (m + 1)],
+                lhsT_scale=v2_scales[m // 4][4 * b : P, P * (m % 4) : P * (m % 4 + 1)],
                 rhs=x_codes[x, b][:, cols].bitcast(FP8X4), rhs_scale=x_scales[x, b][:, cols], start=start, stop=stop,
             )
 
@@ -287,8 +293,8 @@ def tile_list_ramen_topping_scorer_kernel(
             )
             nc.sync.dma_start(out[P * m : P * (m + 1), :], result[:])
 
-        picked = pick_evening(0, 0, f"d2_sb{last}_0")
-        pick_toppings(0, EARLY, M_TILES, f"d2_sb{last}_1")
+        picked = pick_evening(0, 0, f"d2_sb{last}")
+        pick_toppings(0, EARLY, M_TILES, f"picked{last}")
         weave_lunch(1)
         woven0 = keep.tile([P, N, PACK], BF16, name="x2_woven0", tag="x1_planes1", align_bytes=64)
         weave_evening(woven0[:, 0:256, :], picked)
@@ -296,7 +302,7 @@ def tile_list_ramen_topping_scorer_kernel(
         for m in range(3):
             lunch_scores(m)
         weave_evening(woven0[:, 256:N, :], picked)
-        picked = pick_evening(1, 0, f"d2_sb{last}_0")
+        picked = pick_evening(1, 0, f"d2_sb{last}")
         quantise_x(2, 0, woven0, slice(0, N))
         for m in range(3, EARLY):
             lunch_scores(m)

from contextlib import ExitStack

import concourse.mybir as mybir

K, T, S, H, T2, S2, N = 512, 4096, 1024, 1024, 2048, 1024, 512
FLOPS = 2 * (2 * K * H * S) + 2 * (2 * H * S2 * N)

F32 = mybir.dt.float32
BF16 = mybir.dt.bfloat16
I32 = mybir.dt.int32
U32 = mybir.dt.uint32
U16 = mybir.dt.uint16
U8 = mybir.dt.uint8
FP8X4 = mybir.dt.float8_e4m3fn_x4
FP4X4 = mybir.dt.float4_e2m1fn_x4
ACT = mybir.ActivationFunctionType
ALU = mybir.AluOpType

P = 128
PACK = 4
BANK = 512
PASSES = H // (P * PACK)
SLICES = H // P
M_TILES = S2 // P
EARLY = 5


def tile_list_ramen_topping_scorer_kernel(
    tc, tab_words, tab_scales, offs, tab2_words, tab2_scales, offs2, pos1, pos2,
    w1, w4_words, w4_scales, gain, lunch, base, out,
):
    nc = tc.nc
    with ExitStack() as ctx:
        lists = ctx.enter_context(tc.tile_pool(name="lists", bufs=1))
        keep = ctx.enter_context(tc.tile_pool(name="keep", bufs=1))
        psum = ctx.enter_context(tc.psum_pool(name="psum", bufs=1))

        def bank(k, name):
            return psum.tile([P, BANK], F32, name=name, tag=f"bank{k}")

        idx = lists.tile([P, S // 16], U16, name="idx")
        idx2 = lists.tile([P, S2 // 16], U16, name="idx2")
        p1 = lists.tile([P, N // 16], U16, name="p1")
        p2 = lists.tile([P, N // 16], U16, name="p2")

        v_plane = keep.tile([P, T], U8, name="v_plane", tag="v_plane", align_bytes=64)
        v2_plane = keep.tile([P, T2], U8, name="v2_plane", tag="v2_plane", align_bytes=64)
        w4_plane = keep.tile([P, H], U8, name="w4_plane", tag="w4_plane", align_bytes=64)
        v_scales = keep.tile([P, S], U8, name="v_scales", align_bytes=64)
        nc.gpsimd.memset(w4_plane[:].bitcast(I32), 0)
        nc.vector.memset(v2_plane[:].bitcast(I32), 0)
        nc.vector.memset(v_plane[0:112, :].bitcast(I32), 0)
        nc.vector.memset(v_scales[:].bitcast(I32), 0)

        gain_sb = keep.tile([P, PASSES, PACK], F32, name="gain_sb")
        lunch_sb = keep.tile([P, PASSES, PACK], F32, name="lunch_sb")
        w4_raw = keep.tile([P, 2 * H], U8, name="w4_raw", tag="w4_raw", align_bytes=64)
        v_table = keep.tile([P, T], I32, name="v_table", tag="v_table", align_bytes=64)
        w1_rows = w1.rearrange("(p j) c -> p j c", j=PACK)
        w1_raw = {}

        def load_w1(b):
            for u in range(2):
                w1_raw[b, u] = keep.tile([P, PACK, 256], F32, name=f"w1_raw{b}{u}", tag=(("w1_raw00", "w1_raw01"), ("w1_raw00", "v_table"))[b][u], align_bytes=64)
                nc.sync.dma_start(w1_raw[b, u][:], w1_rows[:, :, 512 * b + 256 * u : 512 * b + 256 * (u + 1)])

        nc.sync.dma_start(idx[:], offs)
        nc.sync.dma_start(v_plane[112:P, :].bitcast(I32), tab_scales[0].bitcast(I32))
        nc.sync.dma_start(w4_raw[:].bitcast(I32), w4_words[0].bitcast(I32))
        nc.sync.dma_start(gain_sb[:], gain.rearrange("(b p t) -> p b t", p=P, t=PACK))
        nc.sync.dma_start(idx2[:], offs2)
        nc.sync.dma_start(v_table[:], tab_words[0].rearrange("p t i -> p (t i)").bitcast(I32))
        load_w1(0)
        nc.sync.dma_start(p1[:], pos1)
        nc.sync.dma_start(p2[:], pos2)
        for q in range(4):
            nc.sync.dma_start(v2_plane[32 * q : 32 * q + 8, :].bitcast(I32), tab2_scales[:, 4 * q : 4 * q + 4, :].bitcast(I32))
        for q in range(4):
            nc.gpsimd.dma_start(w4_plane[32 * q : 32 * q + 4, :].bitcast(I32), w4_scales[0, 4 * q : 4 * q + 4, :].bitcast(I32))
        nc.gpsimd.dma_start(lunch_sb[:], lunch.rearrange("(b p t) -> p b t", p=P, t=PACK))

        v2_table = []

        def load_v2_table(a):
            v2_table.append(keep.tile([P, T2], I32, name=f"v2_table{a}", tag=("v_plane", "v2_plane")[a], align_bytes=64))
            nc.sync.dma_start(v2_table[a][:], tab2_words[a].rearrange("p t i -> p (t i)").bitcast(I32))

        gain_abs = keep.tile([P, SLICES], F32, name="gain_abs")
        gain_sign = keep.tile([P, SLICES], F32, name="gain_sign")
        gain_cols = gain_sb[:].rearrange("p b t -> p (b t)")
        lunch_cols = lunch_sb[:].rearrange("p b t -> p (b t)")
        nc.scalar.activation(gain_abs[:], gain_cols, ACT.Abs)
        nc.scalar.activation(gain_sign[:], gain_cols, ACT.Sign)

        v_rows = keep.tile([P, S], U8, name="v_rows", align_bytes=64)
        nc.vector.tensor_copy(v_rows[:], v_plane[:].indirect(idx[:]))
        for q in range(4):
            nc.sync.dma_start(v_scales[32 * q : 32 * q + 4, :].bitcast(I32), v_rows[112 + 4 * q : 116 + 4 * q, :].bitcast(I32))
        v_words = keep.tile([P, S], U32, name="v_words", align_bytes=64)
        for half in range(2):
            nc.vector.tensor_copy(
                v_words[:, BANK * half : BANK * (half + 1)],
                v_table[:].bitcast(U32).indirect(idx[:, 32 * half : 32 * (half + 1)]),
            )

        w4_codes = keep.tile([P, 2 * H], U8, name="w4_codes", align_bytes=64)
        w4_sc = keep.tile([P, H], U8, name="w4_sc", align_bytes=64)
        nc.vector.tensor_copy(
            w4_codes[:].bitcast(U16).rearrange("p (b t q) -> p b q t", b=PASSES, t=PACK),
            w4_raw[:].bitcast(U16).rearrange("p (b q t) -> p b q t", b=PASSES, t=PACK),
        )
        nc.vector.tensor_copy(
            w4_sc[:].rearrange("p (b t q) -> p b q t", b=PASSES, t=PACK),
            w4_plane[:].rearrange("p (b q t) -> p b q t", b=PASSES, t=PACK),
        )

        w1_codes, w1_scales = [], []

        w1_grouped = []

        def cast_w1(b):
            grouped = keep.tile([P, PACK, P, PACK], BF16, name=f"w1_grouped{b}", tag=("w1_grouped0", "w1_raw01")[b], align_bytes=64)
            for u in range(2):
                nc.scalar.copy(
                    grouped[:].rearrange("p t m j -> p m j t")[:, 64 * u : 64 * (u + 1), :, :],
                    w1_raw[b, u][:].rearrange("p j (m t) -> p m j t", t=PACK),
                )
            w1_grouped.append(grouped)

        def quantise_w1(b):
            w1_codes.append(keep.tile([P, BANK], U32, name=f"w1_codes{b}", tag=("w1_codes0", "d2_sb2")[b], align_bytes=64))
            w1_scales.append(keep.tile([P, BANK], U8, name=f"w1_scales{b}", align_bytes=64))
            nc.vector.quantize_mx(
                out=w1_codes[b][:].bitcast(FP8X4), scales=w1_scales[b][:],
                in_=w1_grouped[b][:].rearrange("p t m j -> p (t m j)"),
            )

        v2_scales = []

        def pick_v2_scales(half):
            v2_scales.append(keep.tile([P, S2 // 2], U8, name=f"v2_scales{half}", tag=("v2_scales0", "w1_grouped0")[half], align_bytes=64))
            nc.vector.tensor_copy(v2_scales[half][:], v2_plane[:].indirect(idx2[:, 32 * half : 32 * (half + 1)]))

        pick_v2_scales(0)
        cast_w1(0)
        quantise_w1(0)
        pick_v2_scales(1)
        load_v2_table(0)
        load_w1(1)
        load_v2_table(1)

        d1_banks, d2_sb, h_sb = {}, {}, {}

        def second_features(s):
            d2_sb[s] = keep.tile([P, S], F32, name=f"d2_sb{s}", tag=f"d2_sb{s}" if s else "w1_raw01", align_bytes=64)
            for half in range(2):
                cols = slice(BANK * half, BANK * (half + 1))
                d2 = bank(half, f"d2_{s}_{half}")
                nc.tensor.matmul_mx(
                    out=d2[:], lhsT=w4_codes[:, 2 * P * s : 2 * P * (s + 1)].bitcast(FP4X4), lhsT_scale=w4_sc[:, P * s : P * (s + 1)],
                    rhs=v_words[:, cols].bitcast(FP8X4), rhs_scale=v_scales[:, cols], start=True, stop=True,
                )
                nc.scalar.activation(d2_sb[s][:, cols], d2[:], ACT.Copy, scale=gain_abs[:, s : s + 1])

        def first_features(s):
            b, t = divmod(s, PACK)
            for half in range(2):
                cols = slice(BANK * half, BANK * (half + 1))
                d1 = bank(2 + 2 * (s % 3) + half, f"d1_{s}_{half}")
                nc.tensor.matmul_mx(
                    out=d1[:], lhsT=w1_codes[b][:, P * t : P * (t + 1)].bitcast(FP8X4), lhsT_scale=w1_scales[b][:, P * t : P * (t + 1)],
                    rhs=v_words[:, cols].bitcast(FP8X4), rhs_scale=v_scales[:, cols], start=True, stop=True,
                )
                d1_banks[s, half] = d1

        def first_maximum(s):
            h_sb[s] = keep.tile([P, S], F32, name=f"h_sb{s}")
            for half in range(2):
                cols = slice(BANK * half, BANK * (half + 1))
                nc.vector.scalar_tensor_tensor(
                    out=h_sb[s][:, cols], in0=d1_banks[s, half][:], scalar=gain_abs[:, s : s + 1],
                    in1=d2_sb[s][:, cols], op0=ALU.mult, op1=ALU.max,
                )

        x1_planes = [keep.tile([P, PACK, N], BF16, name=f"x1_planes{b}", tag=f"x1_planes{b}", align_bytes=64) for b in range(PASSES)]

        def pick_lunch(s):
            b, t = divmod(s, PACK)
            picked = keep.tile([P, N], F32, name=f"picked{s}", tag=f"picked{s}", align_bytes=64)
            nc.vector.tensor_copy(picked[:], h_sb[s][:].indirect(p1[:]))
            nc.scalar.activation(
                x1_planes[b][:, t, :], picked[:], ACT.Identity, scale=gain_sign[:, s : s + 1], bias=lunch_cols[:, s : s + 1],
            )

        x_codes = {(x, b): keep.tile([P, N], U32, name=f"x{x}_codes{b}", align_bytes=64) for x in (1, 2) for b in range(PASSES)}
        x_scales = {(x, b): keep.tile([P, N], U8, name=f"x{x}_scales{b}", align_bytes=64) for x in (1, 2) for b in range(PASSES)}

        def quantise_x(x, b, woven, cols):
            nc.vector.quantize_mx(
                out=x_codes[x, b][:, cols].bitcast(FP8X4), scales=x_scales[x, b][:, cols],
                in_=woven[:].rearrange("p n t -> p (n t)"),
            )

        def weave_lunch(b):
            woven = keep.tile([P, N, PACK], BF16, name=f"x1_woven{b}", tag=f"x1_woven{b}", align_bytes=64)
            nc.scalar.copy(
                woven[:].rearrange("p (c i) t -> p c t i", i=4),
                x1_planes[b][:].rearrange("p t (c i) -> p c t i", i=4),
            )
            quantise_x(1, b, woven, slice(0, N))

        def pick_evening(b, half, tag):
            picked = keep.tile([P, PACK, N // 2], F32, name=f"evening{b}_{half}", tag=tag, align_bytes=64)
            for t in range(PACK):
                nc.vector.tensor_copy(picked[:, t, :], h_sb[PACK * b + t][:].indirect(p2[:, 16 * half : 16 * (half + 1)]))
            return picked

        def weave_evening(woven, picked):
            nc.scalar.activation(
                woven.rearrange("p (c i) t -> p c t i", i=4),
                picked[:].rearrange("p t (c i) -> p c t i", i=4),
                ACT.Abs,
            )

        v2_words = {}

        def pick_toppings(a, m0, m1, tag):
            words = keep.tile([P, P * (m1 - m0)], U32, name=f"v2_words{a}_{m0}", tag=tag, align_bytes=64)
            nc.vector.tensor_copy(words[:], v2_table[a][:].bitcast(U32).indirect(idx2[:, 8 * m0 : 8 * m1]))
            for m in range(m0, m1):
                v2_words[a, m] = words[:, P * (m - m0) : P * (m - m0 + 1)]

        for s in range(2):
            second_features(s)
            first_features(s)
        first_features(2)
        first_maximum(0)
        cast_w1(1)
        for s in range(2, SLICES):
            second_features(s)
        for s in range(SLICES):
            if s > 0:
                first_maximum(s)
            if s == 0:
                first_features(3)
            if s == 2:
                quantise_w1(1)
                first_features(4)
            if 2 <= s < SLICES - 3:
                first_features(s + 3)
            pick_lunch(s)
            if s == 1:
                pick_toppings(0, 0, EARLY, "d2_sb1")
            if s == PACK - 1:
                pick_toppings(1, 0, EARLY, "d2_sb3")
                weave_lunch(0)

        base_sb = keep.tile([P, M_TILES], F32, name="base_sb", tag="d2_sb4", align_bytes=64)
        with nc.allow_non_contiguous_dma(reason="one base value to a partition"):
            nc.sync.dma_start(base_sb[:], base.rearrange("(c p) -> p c", p=P))

        last = SLICES - 1

        def second_pass(acc, x, b, m, cols, start, stop):
            nc.tensor.matmul_mx(
                out=acc[:, cols], lhsT=v2_words[b, m].bitcast(FP8X4),
                lhsT_scale=v2_scales[m // 4][4 * b : P, P * (m % 4) : P * (m % 4 + 1)],
                rhs=x_codes[x, b][:, cols].bitcast(FP8X4), rhs_scale=x_scales[x, b][:, cols], start=start, stop=stop,
            )

        e1_sb = []
        e_banks = (0, 1, 6, 7, 2, 3, 4, 5)

        def lunch_scores(m):
            e1 = bank(e_banks[m], f"e1_{m}")
            for b in range(PASSES):
                second_pass(e1, 1, b, m, slice(0, N), b == 0, b == PASSES - 1)
            e1_sb.append(keep.tile([P, N], F32, name=f"e1_sb{m}"))
            nc.scalar.activation(e1_sb[m][:], e1[:], ACT.Identity, bias=base_sb[:, m : m + 1])

        e2_banks = {}

        def open_evening_scores(m):
            e2_banks[m] = bank(e_banks[m], f"e2_{m}")
            second_pass(e2_banks[m], 2, 0, m, slice(0, N), True, False)
            second_pass(e2_banks[m], 2, 1, m, slice(0, 256), False, False)

        def close_evening_scores(m):
            second_pass(e2_banks[m], 2, 1, m, slice(256, N), False, True)
            result = keep.tile([P, N], F32, name=f"result{m}")
            nc.vector.scalar_tensor_tensor(
                out=result[:], in0=e2_banks[m][:], scalar=base_sb[:, m : m + 1], in1=e1_sb[m][:], op0=ALU.add, op1=ALU.max,
            )
            nc.sync.dma_start(out[P * m : P * (m + 1), :], result[:])

        picked = pick_evening(0, 0, f"d2_sb{last}")
        pick_toppings(0, EARLY, M_TILES, f"picked{last}")
        weave_lunch(1)
        woven0 = keep.tile([P, N, PACK], BF16, name="x2_woven0", tag="x1_planes1", align_bytes=64)
        weave_evening(woven0[:, 0:256, :], picked)
        picked = pick_evening(0, 1, "x1_woven1")
        for m in range(3):
            lunch_scores(m)
        weave_evening(woven0[:, 256:N, :], picked)
        picked = pick_evening(1, 0, f"d2_sb{last}")
        quantise_x(2, 0, woven0, slice(0, N))
        for m in range(3, EARLY):
            lunch_scores(m)
        woven1 = [keep.tile([P, N // 2, PACK], BF16, name=f"x2_woven1_{half}", tag=f"x2_woven1_{half}", align_bytes=64) for half in range(2)]
        weave_evening(woven1[0][:], picked)
        picked = pick_evening(1, 1, "x1_planes1")
        quantise_x(2, 1, woven1[0], slice(0, 256))
        pick_toppings(1, EARLY, M_TILES, "x2_woven1_0")
        for m in range(EARLY):
            open_evening_scores(m)
        weave_evening(woven1[1][:], picked)
        quantise_x(2, 1, woven1[1], slice(256, N))
        for m in range(M_TILES):
            if EARLY <= m + 3 < M_TILES:
                lunch_scores(m + 3)
                open_evening_scores(m + 3)
            close_evening_scores(m)
